import numpy as np
import ml_dtypes


def mxq(x, axis, fmt="e4m3"):
    dtype, down = {"e4m3": (ml_dtypes.float8_e4m3fn, 7), "e5m2": (ml_dtypes.float8_e5m2, 14)}[fmt]
    v = np.moveaxis(np.asarray(x, np.float32).astype(ml_dtypes.bfloat16).astype(np.float64), axis, -1)
    blocks = v.reshape(v.shape[:-1] + (-1, 32))
    amax = np.abs(blocks).max(-1, keepdims=True)
    byte = np.maximum(np.where(amax > 0, np.frexp(amax)[1] - 1 + 127, 0) - down, 1)
    scale = np.exp2(byte - 127.0)
    codes = (blocks / scale).astype(np.float32).astype(dtype).astype(np.float64)
    return np.moveaxis((codes * scale).reshape(v.shape), -1, axis)


WIDE = False


def mx_kscale(k):
    if not WIDE:
        return np.ones(k)
    levels = np.array([10, -10, 5, -5, 0])
    if k % 512:
        return np.exp2(np.random.permutation(np.resize(levels, k // 32))).repeat(32)
    a = np.empty((k // 512, 16))
    for p in range(k // 512):
        a[p, :8] = np.random.permutation(np.resize(levels, 8))
        for g in range(8):
            far = levels[np.abs(levels - a[p, g]) >= 10]
            a[p, g + 8] = far[np.random.randint(len(far))]
    return np.exp2(a.ravel()).repeat(32)


def f64(x):
    return np.asarray(x).astype(np.float64)


def striped(idx):
    return np.tile(np.asarray(idx).reshape(-1, 16).T, (8, 1)).astype(np.uint16)


def unstriped(offs):
    return offs[:16].T.reshape(-1).astype(np.int64)


def striped8(idx):
    return np.asarray(idx).reshape(8, -1, 16).transpose(0, 2, 1).reshape(128, -1).astype(np.uint16)


def unstriped8(offs):
    return offs.reshape(8, 16, -1).transpose(0, 2, 1).reshape(8, -1).astype(np.int64)


def pick8(x, idx, run):
    r = np.arange(len(x))
    return x[r[:, None], idx[r % (8 * run) // run]]


E2M1 = np.array([0.0, 0.5, 1.0, 1.5, 2.0, 3.0, 4.0, 6.0, -0.0, -0.5, -1.0, -1.5, -2.0, -3.0, -4.0, -6.0])


def pack_weight(w, fmt):
    k, n = w.shape
    w = f64(np.asarray(w, np.float32).astype(ml_dtypes.bfloat16)).reshape(k // 32, 32, n)
    amax = np.abs(w).max(1)
    if fmt == "e4m3":
        byte = np.frexp(amax)[1] - 1 + 127 - 7
    else:
        mant, ex = np.frexp(amax / 6.0)
        byte = np.where(mant > 0.5, ex, ex - 1) + 127
    byte = np.clip(np.where(amax > 0, byte, 1), 1, 254)
    scaled = (w * np.exp2(127.0 - byte)[:, None, :]).reshape(k, n).astype(np.float32)
    by_word = np.ascontiguousarray(scaled.reshape(k // 512, 128, 4, n).transpose(0, 1, 3, 2))
    if fmt == "e4m3":
        words = by_word.astype(ml_dtypes.float8_e4m3fn).view(np.uint8)
    else:
        c = by_word.astype(ml_dtypes.float4_e2m1fn).view(np.uint8) & 0xF
        words = (c[..., 0::2] | (c[..., 1::2] << 4)).reshape(k // 512, 128, 2 * n)
    return np.ascontiguousarray(words), np.ascontiguousarray(byte.astype(np.uint8).reshape(k // 512, 16, n))


def unpack_weight(words, scales, fmt):
    g, _, n = scales.shape
    words = np.ascontiguousarray(words).reshape(g, 128, n, -1)
    if fmt == "e4m3":
        vals = words.view(ml_dtypes.float8_e4m3fn).astype(np.float64)
    else:
        nib = np.empty((g, 128, n, 4), np.uint8)
        nib[..., 0::2] = words & 0xF
        nib[..., 1::2] = words >> 4
        vals = E2M1[nib]
    vals = vals * np.repeat(np.exp2(scales.astype(np.float64) - 127.0), 8, axis=1)[..., None]
    return vals.transpose(0, 1, 3, 2).reshape(g * 512, n)


K, J, R, T, Z, M, C, S, N, V = 512, 512, 512, 2048, 512, 1024, 1024, 256, 256, 1024


def setup_inputs():
    n = np.random.standard_normal
    idx = np.random.permutation(T)[:J]
    idx2 = np.random.permutation(M)[:J]
    idx3 = np.stack([np.random.permutation(C)[:J] for _ in range(8)])
    idx4 = np.stack([np.random.permutation(C)[:S] for _ in range(8)])
    idx5 = np.stack([np.random.permutation(J)[:S] for _ in range(8)])
    idx6 = np.random.permutation(V)[:N]
    fk = mx_kscale(K)
    fr = mx_kscale(R)
    fz = mx_kscale(Z)
    xtp = pack_weight(n((K, T)) * fk[:, None], "e4m3")
    wp = pack_weight(n((K, R)) * 1 / np.sqrt(K) / fk[:, None] * fr, "e2m1")
    xop = pack_weight(n((Z, M)) / fz[:, None], "e2m1")
    w2p = pack_weight(n((Z, R)) * 1 / np.sqrt(Z) * fz[:, None] * fr, "e4m3")
    vsp = pack_weight(n((R, V)) * 1 / np.sqrt(R) / fr[:, None], "e4m3")
    return {
        "xt_words": xtp[0],
        "xt_scales": xtp[1],
        "w_words": wp[0],
        "w_scales": wp[1],
        "xo_words": xop[0],
        "xo_scales": xop[1],
        "w2_words": w2p[0],
        "w2_scales": w2p[1],
        "sa": (np.random.uniform(0.5, 1.6, (R, 1))).astype(np.float32),
        "vs_words": vsp[0],
        "vs_scales": vsp[1],
        "offs": striped(idx),
        "offs2": striped(idx2),
        "offs3": striped8(idx3),
        "offs4": striped8(idx4),
        "offs5": striped8(idx5),
        "offs6": striped(idx6),
    }


def reference(xt_words, xt_scales, w_words, w_scales, xo_words, xo_scales, w2_words, w2_scales, sa, vs_words, vs_scales, offs, offs2, offs3, offs4, offs5, offs6):
    idx = unstriped(offs)
    idx2 = unstriped(offs2)
    idx3 = unstriped8(offs3)
    idx4 = unstriped8(offs4)
    idx5 = unstriped8(offs5)
    idx6 = unstriped(offs6)
    xtu = unpack_weight(xt_words, xt_scales, "e4m3")
    wu = unpack_weight(w_words, w_scales, "e2m1")
    xou = unpack_weight(xo_words, xo_scales, "e2m1")
    w2u = unpack_weight(w2_words, w2_scales, "e4m3")
    vsu = unpack_weight(vs_words, vs_scales, "e4m3")
    xtidxg = xtu[:, idx]
    a = wu.T @ xtidxg
    xoidx2g = xou[:, idx2]
    b = w2u.T @ xoidx2g
    pw = np.zeros((R, C))
    pw[np.arange(R)[:, None], idx3[np.arange(R) % 512 // 64]] = a
    h1 = pick8(pw, idx4, 64) * f64(sa)
    pv = np.zeros((R, J))
    pv[np.arange(R)[:, None], idx5[np.arange(R) % 512 // 64]] = h1
    hid = np.maximum(b, pv)
    vsidx6g = vsu[:, idx6]
    hidq = mxq(hid, 0, "e4m3")
    y = vsidx6g.T @ hidq
    return y

@@ -1,0 +1,247 @@
+from contextlib import ExitStack
+
+import concourse.mybir as mybir
+
+F32 = mybir.dt.float32
+BF16 = mybir.dt.bfloat16
+I32 = mybir.dt.int32
+U32 = mybir.dt.uint32
+U16 = mybir.dt.uint16
+U8 = mybir.dt.uint8
+FP8X4 = mybir.dt.float8_e4m3fn_x4
+FP4X4 = mybir.dt.float4_e2m1fn_x4
+COPY = mybir.ActivationFunctionType.Copy
+MAX = mybir.AluOpType.max
+
+P = 128
+PACK = 4
+K, J, R, T, Z, M, C, S, N, V = 512, 512, 512, 2048, 512, 1024, 1024, 256, 256, 1024
+LIST_ROWS = 16
+HEAD = 128
+TAIL = 128
+
+FLOPS = 2 * K * R * J + 2 * Z * R * J + 2 * R * N * J
+
+
+def tile_picked_tokens_plain_two_returned_store_plain_kernel(
+    tc, xt_words, xt_scales, w_words, w_scales, xo_words, xo_scales, w2_words, w2_scales, sa,
+    vs_words, vs_scales, offs, offs2, offs3, offs4, offs5, offs6, out,
+):
+    nc = tc.nc
+    with ExitStack() as ctx:
+        lists = ctx.enter_context(tc.tile_pool(name="lists", bufs=1))
+        sb = ctx.enter_context(tc.tile_pool(name="sb", bufs=1))
+        raw = ctx.enter_context(tc.tile_pool(name="raw", bufs=1))
+        mid = ctx.enter_context(tc.tile_pool(name="mid", bufs=1))
+        ps = ctx.enter_context(tc.psum_pool(name="ps", bufs=1))
+
+        def load_list(name, src):
+            tile = lists.tile(list(src.shape), U16, name=name)
+            nc.sync.dma_start(tile[:], src)
+            return tile
+
+        def entries(tile, first, last):
+            return tile[:, first // LIST_ROWS : last // LIST_ROWS]
+
+        def load_e4m3(name, src, cols, offset):
+            tile = raw.tile([P, cols], U32, name=name, offset=offset, align_bytes=64)
+            nc.sync.dma_start(tile[:].bitcast(I32), src[0].rearrange("p n t -> p (n t)").bitcast(I32))
+            return tile
+
+        def load_e2m1(name, src, cols, offset, queue):
+            tile = raw.tile([P, cols], U16, name=name, offset=offset, align_bytes=64)
+            queue.dma_start(tile[:].bitcast(I32), src[0].bitcast(I32))
+            return tile
+
+        def zeroed_plane(name, cols, offset):
+            tile = raw.tile([P, cols], U8, name=name, offset=offset, align_bytes=64)
+            nc.vector.memset(tile[:].bitcast(I32), 0)
+            return tile
+
+        def load_plane(queue, tile, src):
+            for q in range(4):
+                queue.dma_start(tile[32 * q : 32 * q + 4, :].bitcast(I32), src[0, 4 * q : 4 * q + 4, :].bitcast(I32))
+
+        def bank(b, shape):
+            return ps.tile(shape, F32, name=f"bank{b}", tag=f"bank{b}")
+
+        xt_plane = zeroed_plane("xt_plane", T, 8192)
+        w_plane = zeroed_plane("w_plane", R, 10240)
+        w_rows = sb.tile([4, 4, R // 4], I32, name="w_rows")
+        w_raw = load_e2m1("w_raw", w_words, R, 10752, nc.scalar)
+        nc.scalar.dma_start(w_rows[:], w_scales[0].rearrange("(q r) n -> r q n", r=4).bitcast(I32))
+        load_plane(nc.scalar, xt_plane, xt_scales)
+        gain = sb.tile([P, PACK], F32, name="gain")
+        nc.gpsimd.dma_start(gain[:], sa.rearrange("(p t) o -> p (t o)", t=PACK))
+        idx = load_list("idx", offs)
+        idx3 = load_list("idx3", offs3)
+        idx4 = load_list("idx4", offs4)
+        xt_raw = load_e4m3("xt_raw", xt_words, T, 0)
+        idx5 = load_list("idx5", offs5)
+        idx2 = load_list("idx2", offs2)
+        idx6 = load_list("idx6", offs6)
+
+        boards = [sb.tile([P, C], F32, name=f"board{i}") for i in range(2)]
+        for board in boards:
+            nc.vector.memset(board[:], 0.0)
+
+        for q in range(4):
+            nc.vector.tensor_copy(out=w_plane[32 * q : 32 * q + 4, :].bitcast(I32), in_=w_rows[:, q, :])
+        w_code = mid.tile([P, PACK, P], U16, name="w_code", offset=2048, align_bytes=64)
+        w_scale = mid.tile([P, PACK, P], U8, name="w_scale", offset=3072, align_bytes=64)
+        nc.scalar.copy(out=w_code[:], in_=w_raw[:].rearrange("p (m t) -> p t m", t=PACK))
+        nc.vector.tensor_copy(out=w_scale[:], in_=w_plane[:].rearrange("p (m t) -> p t m", t=PACK))
+
+        x_code = mid.tile([P, J], U32, name="x_code", offset=0, align_bytes=64)
+        x_scale = mid.tile([P, J], U8, name="x_scale", offset=3584, align_bytes=64)
+        nc.vector.tensor_copy(out=x_scale[:, : J // 2], in_=xt_plane[:].indirect(entries(idx, 0, J // 2)))
+        nc.vector.tensor_copy(out=x_code[:, :HEAD], in_=xt_raw[:].indirect(entries(idx, 0, HEAD)))
+        nc.vector.tensor_copy(out=x_scale[:, J // 2 :], in_=xt_plane[:].indirect(entries(idx, J // 2, J)))
+        nc.vector.tensor_copy(out=x_code[:, HEAD:], in_=xt_raw[:].indirect(entries(idx, HEAD, J)))
+
+        def first_product(dst, t, first, last):
+            nc.tensor.matmul_mx(
+                dst, lhsT=w_code[:, t, :].bitcast(FP4X4), lhsT_scale=w_scale[:, t, :],
+                rhs=x_code[:, first:last].bitcast(FP8X4), rhs_scale=x_scale[:, first:last],
+                start=True, stop=True,
+            )
+
+        a_head = []
+        for t in range(2):
+            acc = bank(t, [P, HEAD])
+            first_product(acc[:], t, 0, HEAD)
+            head = mid.tile([P, HEAD], F32, name=f"a_head{t}", offset=4096 + 2048 * t, align_bytes=64)
+            nc.scalar.activation(out=head[:], in_=acc[:], func=COPY)
+            a_head.append(head)
+
+        a_rest = []
+        for t in range(2):
+            acc = bank(2 + t, [P, J - HEAD])
+            first_product(acc[:, :HEAD], t, HEAD, 2 * HEAD)
+            first_product(acc[:, HEAD:], t, 2 * HEAD, J)
+            rest = mid.tile([P, J - HEAD], F32, name=f"a_rest{t}", offset=4096 + 2048 * t + 4 * HEAD, align_bytes=64)
+            nc.vector.tensor_copy(out=rest[:], in_=acc[:])
+            a_rest.append(rest)
+        for t in range(2, PACK):
+            acc = bank(2 + t, [P, J])
+            first_product(acc[:], t, 0, J)
+            rest = sb.tile([P, J], F32, name=f"a_rest{t}")
+            nc.vector.tensor_copy(out=rest[:], in_=acc[:])
+            a_rest.append(rest)
+
+        xo_raw = load_e2m1("xo_raw", xo_words, M, 0, nc.sync)
+        w2_raw = load_e4m3("w2_raw", w2_words, R, 2048)
+        xo_plane = zeroed_plane("xo_plane", M, 8192)
+        w2_plane = zeroed_plane("w2_plane", R, 9216)
+        vs_plane = zeroed_plane("vs_plane", V, 9728)
+        load_plane(nc.sync, xo_plane, xo_scales)
+        load_plane(nc.sync, w2_plane, w2_scales)
+        load_plane(nc.sync, vs_plane, vs_scales)
+
+        slots = [mid.tile([P, J], F32, name=f"slots{t}", offset=2048 * t, align_bytes=64) for t in range(PACK)]
+
+        o_code = sb.tile([P, J], U16, name="o_code", align_bytes=64)
+        o_scale = sb.tile([P, J], U8, name="o_scale", align_bytes=64)
+        nc.vector.tensor_copy(out=o_code[:], in_=xo_raw[:].indirect(idx2[:]))
+        nc.vector.tensor_copy(out=o_scale[:], in_=xo_plane[:].indirect(idx2[:]))
+        w2_code = sb.tile([P, PACK, P], U32, name="w2_code", align_bytes=64)
+        w2_scale = sb.tile([P, PACK, P], U8, name="w2_scale", align_bytes=64)
+        nc.vector.tensor_copy(out=w2_code[:], in_=w2_raw[:].rearrange("p (m t) -> p t m", t=PACK))
+        nc.vector.tensor_copy(out=w2_scale[:], in_=w2_plane[:].rearrange("p (m t) -> p t m", t=PACK))
+        vs_raw = load_e4m3("vs_raw", vs_words, V, 4096)
+        b_ps = []
+        for t in range(PACK):
+            acc = bank((6 + t) % 8, [P, J])
+            nc.tensor.matmul_mx(
+                acc[:], lhsT=w2_code[:, t, :].bitcast(FP8X4), lhsT_scale=w2_scale[:, t, :],
+                rhs=o_code[:].bitcast(FP4X4), rhs_scale=o_scale[:], start=True, stop=True,
+            )
+            b_ps.append(acc)
+
+        v_code = sb.tile([P, N], U32, name="v_code", align_bytes=64)
+        v_scale = sb.tile([P, N], U8, name="v_scale", align_bytes=64)
+        nc.vector.tensor_copy(out=v_code[:], in_=vs_raw[:].indirect(idx6[:]))
+        nc.vector.tensor_copy(out=v_scale[:], in_=vs_plane[:].indirect(idx6[:]))
+
+        fetched = [sb.tile([P, S], F32, name=f"fetched{t}") for t in range(PACK)]
+        hid = sb.tile([P, J, PACK], BF16, name="hid", align_bytes=64)
+
+        def put(t, first, last, src):
+            nc.scalar.activation(out=boards[t % 2][:].indirect(entries(idx3, first, last)), in_=src, func=COPY)
+
+        def fetch(t):
+            nc.scalar.activation(
+                out=fetched[t][:], in_=boards[t % 2][:].indirect(idx4[:]), func=COPY, scale=gain[:, t : t + 1]
+            )
+
+        def hand_back(t):
+            nc.scalar.activation(out=slots[t][:].indirect(idx5[:]), in_=fetched[t][:], func=COPY)
+
+        def larger(t, first, last):
+            nc.vector.tensor_tensor(
+                out=hid[:, first:last, t], in0=b_ps[t][:, first:last], in1=slots[t][:, first:last], op=MAX
+            )
+
+        for t in range(2):
+            put(t, 0, HEAD, a_head[t][:])
+        for t in range(2):
+            put(t, HEAD, J, a_rest[t][:])
+        for tile in slots:
+            nc.vector.memset(tile[:], 0.0)
+        fetch(0)
+        fetch(1)
+        put(2, 0, J, a_rest[2][:])
+        hand_back(0)
+        larger(0, 0, J)
+        put(3, 0, J, a_rest[3][:])
+        hand_back(1)
+        larger(1, 0, J)
+        fetch(2)
+        fetch(3)
+        hand_back(2)
+        larger(2, 0, J)
+        hand_back(3)
+
+        h_code = sb.tile([P, J], U32, name="h_code", align_bytes=64)
+        h_scale = sb.tile([P, J], U8, name="h_scale", align_bytes=64)
+        blocks = N // P
+        chunks = J // TAIL
+
+        def finish(c):
+            cols = slice(c * TAIL, (c + 1) * TAIL)
+            nc.vector.quantize_mx(
+                out=h_code[:, cols].bitcast(FP8X4), scales=h_scale[:, cols],
+                in_=hid[:, cols, :].rearrange("p j t -> p (j t)"),
+            )
+
+            def product(dst, b):
+                rows = slice(b * P, (b + 1) * P)
+                nc.tensor.matmul_mx(
+                    dst, lhsT=v_code[:, rows].bitcast(FP8X4), lhsT_scale=v_scale[:, rows],
+                    rhs=h_code[:, cols].bitcast(FP8X4), rhs_scale=h_scale[:, cols], start=True, stop=True,
+                )
+
+            if c < chunks - 1:
+                acc = bank(2 + c, [P, blocks, TAIL])
+                for b in range(blocks):
+                    product(acc[:, b, :], b)
+                result = sb.tile([P, blocks, TAIL], F32, name=f"result{c}")
+                nc.scalar.activation(out=result[:], in_=acc[:], func=COPY)
+                nc.sync.dma_start(out.rearrange("(b p) j -> p b j", p=P)[:, :, cols], result[:])
+                return
+            for b in range(blocks):
+                acc = bank(2 + c + b, [P, TAIL])
+                product(acc[:], b)
+                result = sb.tile([P, TAIL], F32, name=f"last{b}")
+                if b == 0:
+                    nc.scalar.activation(out=result[:], in_=acc[:], func=COPY)
+                    nc.scalar.dma_start(out[b * P : (b + 1) * P, cols], result[:])
+                else:
+                    nc.vector.tensor_copy(out=result[:], in_=acc[:])
+                    nc.sync.dma_start(out[b * P : (b + 1) * P, cols], result[:])
+
+        for c in range(chunks):
+            larger(3, c * TAIL, (c + 1) * TAIL)
+            if c > 0:
+                finish(c - 1)
+        finish(chunks - 1)

@@ -43,9 +43,9 @@ def tile_picked_tokens_plain_two_returned_store_plain_kernel(
         def entries(tile, first, last):
             return tile[:, first // LIST_ROWS : last // LIST_ROWS]
 
-        def load_e4m3(name, src, cols, offset):
+        def load_e4m3(name, src, cols, offset, queue):
             tile = raw.tile([P, cols], U32, name=name, offset=offset, align_bytes=64)
-            nc.sync.dma_start(tile[:].bitcast(I32), src[0].rearrange("p n t -> p (n t)").bitcast(I32))
+            queue.dma_start(tile[:].bitcast(I32), src[0].rearrange("p n t -> p (n t)").bitcast(I32))
             return tile
 
         def load_e2m1(name, src, cols, offset, queue):
@@ -65,21 +65,23 @@ def tile_picked_tokens_plain_two_returned_store_plain_kernel(
         def bank(b, shape):
             return ps.tile(shape, F32, name=f"bank{b}", tag=f"bank{b}")
 
-        xt_plane = zeroed_plane("xt_plane", T, 8192)
+        xt_plane = raw.tile([P, T], U8, name="xt_plane", offset=8192, align_bytes=64)
+        nc.vector.memset(xt_plane[:, : T // 2].bitcast(I32), 0)
+        nc.gpsimd.memset(xt_plane[:, T // 2 :].bitcast(I32), 0)
         w_plane = zeroed_plane("w_plane", R, 10240)
         w_rows = sb.tile([4, 4, R // 4], I32, name="w_rows")
+        nc.sync.dma_start(w_rows[:], w_scales[0].rearrange("(q r) n -> r q n", r=4).bitcast(I32))
         w_raw = load_e2m1("w_raw", w_words, R, 10752, nc.scalar)
-        nc.scalar.dma_start(w_rows[:], w_scales[0].rearrange("(q r) n -> r q n", r=4).bitcast(I32))
-        load_plane(nc.scalar, xt_plane, xt_scales)
-        gain = sb.tile([P, PACK], F32, name="gain")
-        nc.gpsimd.dma_start(gain[:], sa.rearrange("(p t) o -> p (t o)", t=PACK))
+        xt_raw = load_e4m3("xt_raw", xt_words, T, 0, nc.scalar)
+        load_plane(nc.sync, xt_plane, xt_scales)
         idx = load_list("idx", offs)
         idx3 = load_list("idx3", offs3)
         idx4 = load_list("idx4", offs4)
-        xt_raw = load_e4m3("xt_raw", xt_words, T, 0)
         idx5 = load_list("idx5", offs5)
         idx2 = load_list("idx2", offs2)
         idx6 = load_list("idx6", offs6)
+        gain = sb.tile([P, PACK], F32, name="gain")
+        nc.gpsimd.dma_start(gain[:], sa.rearrange("(p t) o -> p (t o)", t=PACK))
 
         boards = [sb.tile([P, C], F32, name=f"board{i}") for i in range(2)]
         for board in boards:
@@ -90,14 +92,16 @@ def tile_picked_tokens_plain_two_returned_store_plain_kernel(
         w_code = mid.tile([P, PACK, P], U16, name="w_code", offset=2048, align_bytes=64)
         w_scale = mid.tile([P, PACK, P], U8, name="w_scale", offset=3072, align_bytes=64)
         nc.scalar.copy(out=w_code[:], in_=w_raw[:].rearrange("p (m t) -> p t m", t=PACK))
-        nc.vector.tensor_copy(out=w_scale[:], in_=w_plane[:].rearrange("p (m t) -> p t m", t=PACK))
+        dealt = w_plane[:].rearrange("p (m t) -> p t m", t=PACK)
+        nc.vector.tensor_copy(out=w_scale[:, :2, :], in_=dealt[:, :2, :])
 
         x_code = mid.tile([P, J], U32, name="x_code", offset=0, align_bytes=64)
         x_scale = mid.tile([P, J], U8, name="x_scale", offset=3584, align_bytes=64)
         nc.vector.tensor_copy(out=x_scale[:, : J // 2], in_=xt_plane[:].indirect(entries(idx, 0, J // 2)))
         nc.vector.tensor_copy(out=x_code[:, :HEAD], in_=xt_raw[:].indirect(entries(idx, 0, HEAD)))
+        nc.vector.tensor_copy(out=x_code[:, HEAD : J // 2], in_=xt_raw[:].indirect(entries(idx, HEAD, J // 2)))
         nc.vector.tensor_copy(out=x_scale[:, J // 2 :], in_=xt_plane[:].indirect(entries(idx, J // 2, J)))
-        nc.vector.tensor_copy(out=x_code[:, HEAD:], in_=xt_raw[:].indirect(entries(idx, HEAD, J)))
+        nc.vector.tensor_copy(out=x_code[:, J // 2 :], in_=xt_raw[:].indirect(entries(idx, J // 2, J)))
 
         def first_product(dst, t, first, last):
             nc.tensor.matmul_mx(
@@ -122,6 +126,7 @@ def tile_picked_tokens_plain_two_returned_store_plain_kernel(
             rest = mid.tile([P, J - HEAD], F32, name=f"a_rest{t}", offset=4096 + 2048 * t + 4 * HEAD, align_bytes=64)
             nc.vector.tensor_copy(out=rest[:], in_=acc[:])
             a_rest.append(rest)
+        nc.vector.tensor_copy(out=w_scale[:, 2:, :], in_=dealt[:, 2:, :])
         for t in range(2, PACK):
             acc = bank(2 + t, [P, J])
             first_product(acc[:], t, 0, J)
@@ -130,7 +135,7 @@ def tile_picked_tokens_plain_two_returned_store_plain_kernel(
             a_rest.append(rest)
 
         xo_raw = load_e2m1("xo_raw", xo_words, M, 0, nc.sync)
-        w2_raw = load_e4m3("w2_raw", w2_words, R, 2048)
+        w2_raw = load_e4m3("w2_raw", w2_words, R, 2048, nc.sync)
         xo_plane = zeroed_plane("xo_plane", M, 8192)
         w2_plane = zeroed_plane("w2_plane", R, 9216)
         vs_plane = zeroed_plane("vs_plane", V, 9728)
@@ -148,7 +153,7 @@ def tile_picked_tokens_plain_two_returned_store_plain_kernel(
         w2_scale = sb.tile([P, PACK, P], U8, name="w2_scale", align_bytes=64)
         nc.vector.tensor_copy(out=w2_code[:], in_=w2_raw[:].rearrange("p (m t) -> p t m", t=PACK))
         nc.vector.tensor_copy(out=w2_scale[:], in_=w2_plane[:].rearrange("p (m t) -> p t m", t=PACK))
-        vs_raw = load_e4m3("vs_raw", vs_words, V, 4096)
+        vs_raw = load_e4m3("vs_raw", vs_words, V, 4096, nc.sync)
         b_ps = []
         for t in range(PACK):
             acc = bank((6 + t) % 8, [P, J])
@@ -240,8 +245,11 @@ def tile_picked_tokens_plain_two_returned_store_plain_kernel(
                     nc.vector.tensor_copy(out=result[:], in_=acc[:])
                     nc.sync.dma_start(out[b * P : (b + 1) * P, cols], result[:])
 
-        for c in range(chunks):
+        half = J // 2
+        plain = sb.tile([P, half], BF16, name="plain")
+        nc.vector.tensor_tensor(out=plain[:], in0=b_ps[3][:, half:], in1=slots[3][:, half:], op=MAX)
+        for c in range(2):
+            nc.scalar.copy(out=hid[:, half + c * TAIL : half + (c + 1) * TAIL, 3], in_=plain[:, c * TAIL : (c + 1) * TAIL])
             larger(3, c * TAIL, (c + 1) * TAIL)
-            if c > 0:
-                finish(c - 1)
-        finish(chunks - 1)
+        for c in range(chunks):
+            finish(c)

@@ -59,8 +59,9 @@ def tile_picked_tokens_plain_two_returned_store_plain_kernel(
             return tile
 
         def load_plane(queue, tile, src):
-            for q in range(4):
-                queue.dma_start(tile[32 * q : 32 * q + 4, :].bitcast(I32), src[0, 4 * q : 4 * q + 4, :].bitcast(I32))
+            rows = src[0].rearrange("(q r) n -> r q n", r=4)
+            for r in range(4):
+                queue.dma_start(tile[r:P:32, :].bitcast(I32), rows[r].bitcast(I32))
 
         def bank(b, shape):
             return ps.tile(shape, F32, name=f"bank{b}", tag=f"bank{b}")

@@ -81,8 +81,6 @@ def tile_picked_tokens_plain_two_returned_store_plain_kernel(
         idx5 = load_list("idx5", offs5)
         idx2 = load_list("idx2", offs2)
         idx6 = load_list("idx6", offs6)
-        gain = sb.tile([P, PACK], F32, name="gain")
-        nc.gpsimd.dma_start(gain[:], sa.rearrange("(p t) o -> p (t o)", t=PACK))
 
         boards = [sb.tile([P, C], F32, name=f"board{i}") for i in range(2)]
         for board in boards:
@@ -135,6 +133,8 @@ def tile_picked_tokens_plain_two_returned_store_plain_kernel(
             nc.vector.tensor_copy(out=rest[:], in_=acc[:])
             a_rest.append(rest)
 
+        gain = raw.tile([P, PACK], F32, name="gain", offset=10752, align_bytes=64)
+        nc.sync.dma_start(gain[:], sa.rearrange("(p t) o -> p (t o)", t=PACK))
         xo_raw = load_e2m1("xo_raw", xo_words, M, 0, nc.sync)
         w2_raw = load_e4m3("w2_raw", w2_words, R, 2048, nc.sync)
         xo_plane = zeroed_plane("xo_plane", M, 8192)

@@ -99,8 +99,6 @@ def tile_picked_tokens_plain_two_returned_store_plain_kernel(
         nc.vector.tensor_copy(out=x_scale[:, : J // 2], in_=xt_plane[:].indirect(entries(idx, 0, J // 2)))
         nc.vector.tensor_copy(out=x_code[:, :HEAD], in_=xt_raw[:].indirect(entries(idx, 0, HEAD)))
         nc.vector.tensor_copy(out=x_code[:, HEAD : J // 2], in_=xt_raw[:].indirect(entries(idx, HEAD, J // 2)))
-        nc.vector.tensor_copy(out=x_scale[:, J // 2 :], in_=xt_plane[:].indirect(entries(idx, J // 2, J)))
-        nc.vector.tensor_copy(out=x_code[:, J // 2 :], in_=xt_raw[:].indirect(entries(idx, J // 2, J)))
 
         def first_product(dst, t, first, last):
             nc.tensor.matmul_mx(
@@ -113,21 +111,27 @@ def tile_picked_tokens_plain_two_returned_store_plain_kernel(
         for t in range(2):
             acc = bank(t, [P, HEAD])
             first_product(acc[:], t, 0, HEAD)
-            head = mid.tile([P, HEAD], F32, name=f"a_head{t}", offset=4096 + 2048 * t, align_bytes=64)
+            head = mid.tile([P, HEAD], F32, name=f"a_head{t}", offset=4096 + 512 * t, align_bytes=64)
             nc.scalar.activation(out=head[:], in_=acc[:], func=COPY)
             a_head.append(head)
 
+        acc = bank(2, [P, 2, HEAD])
+        for t in range(2):
+            first_product(acc[:, t, :], t, HEAD, 2 * HEAD)
+        a_next = mid.tile([P, 2, HEAD], F32, name="a_next", offset=5120, align_bytes=64)
+        nc.vector.tensor_copy(out=a_next[:], in_=acc[:])
+        nc.vector.tensor_copy(out=x_scale[:, J // 2 :], in_=xt_plane[:].indirect(entries(idx, J // 2, J)))
+        nc.vector.tensor_copy(out=x_code[:, J // 2 :], in_=xt_raw[:].indirect(entries(idx, J // 2, J)))
         a_rest = []
         for t in range(2):
-            acc = bank(2 + t, [P, J - HEAD])
-            first_product(acc[:, :HEAD], t, HEAD, 2 * HEAD)
-            first_product(acc[:, HEAD:], t, 2 * HEAD, J)
-            rest = mid.tile([P, J - HEAD], F32, name=f"a_rest{t}", offset=4096 + 2048 * t + 4 * HEAD, align_bytes=64)
+            acc = bank(3 + t, [P, J // 2])
+            first_product(acc[:], t, J // 2, J)
+            rest = mid.tile([P, J // 2], F32, name=f"a_rest{t}", offset=6144 + 1024 * t, align_bytes=64)
             nc.vector.tensor_copy(out=rest[:], in_=acc[:])
             a_rest.append(rest)
         nc.vector.tensor_copy(out=w_scale[:, 2:, :], in_=dealt[:, 2:, :])
         for t in range(2, PACK):
-            acc = bank(2 + t, [P, J])
+            acc = bank(3 + t, [P, J])
             first_product(acc[:], t, 0, J)
             rest = sb.tile([P, J], F32, name=f"a_rest{t}")
             nc.vector.tensor_copy(out=rest[:], in_=acc[:])
@@ -157,7 +161,7 @@ def tile_picked_tokens_plain_two_returned_store_plain_kernel(
         vs_raw = load_e4m3("vs_raw", vs_words, V, 4096, nc.sync)
         b_ps = []
         for t in range(PACK):
-            acc = bank((6 + t) % 8, [P, J])
+            acc = bank((7 + t) % 8, [P, J])
             nc.tensor.matmul_mx(
                 acc[:], lhsT=w2_code[:, t, :].bitcast(FP8X4), lhsT_scale=w2_scale[:, t, :],
                 rhs=o_code[:].bitcast(FP4X4), rhs_scale=o_scale[:], start=True, stop=True,
@@ -191,7 +195,9 @@ def tile_picked_tokens_plain_two_returned_store_plain_kernel(
         for t in range(2):
             put(t, 0, HEAD, a_head[t][:])
         for t in range(2):
-            put(t, HEAD, J, a_rest[t][:])
+            put(t, HEAD, 2 * HEAD, a_next[:, t, :])
+        for t in range(2):
+            put(t, J // 2, J, a_rest[t][:])
         for tile in slots:
             nc.vector.memset(tile[:], 0.0)
         fetch(0)
@@ -228,7 +234,7 @@ def tile_picked_tokens_plain_two_returned_store_plain_kernel(
                 )
 
             if c < chunks - 1:
-                acc = bank(2 + c, [P, blocks, TAIL])
+                acc = bank(3 + c, [P, blocks, TAIL])
                 for b in range(blocks):
                     product(acc[:, b, :], b)
                 result = sb.tile([P, blocks, TAIL], F32, name=f"result{c}")
@@ -236,7 +242,7 @@ def tile_picked_tokens_plain_two_returned_store_plain_kernel(
                 nc.sync.dma_start(out.rearrange("(b p) j -> p b j", p=P)[:, :, cols], result[:])
                 return
             for b in range(blocks):
-                acc = bank(2 + c + b, [P, TAIL])
+                acc = bank(3 + c + b, [P, TAIL])
                 product(acc[:], b)
                 result = sb.tile([P, TAIL], F32, name=f"last{b}")
                 if b == 0:

from contextlib import ExitStack

import concourse.mybir as mybir

F32 = mybir.dt.float32
BF16 = mybir.dt.bfloat16
I32 = mybir.dt.int32
U32 = mybir.dt.uint32
U16 = mybir.dt.uint16
U8 = mybir.dt.uint8
FP8X4 = mybir.dt.float8_e4m3fn_x4
FP4X4 = mybir.dt.float4_e2m1fn_x4
COPY = mybir.ActivationFunctionType.Copy
MAX = mybir.AluOpType.max

P = 128
PACK = 4
K, J, R, T, Z, M, C, S, N, V = 512, 512, 512, 2048, 512, 1024, 1024, 256, 256, 1024
LIST_ROWS = 16
HEAD = 128
TAIL = 128

FLOPS = 2 * K * R * J + 2 * Z * R * J + 2 * R * N * J


def tile_picked_tokens_plain_two_returned_store_plain_kernel(
    tc, xt_words, xt_scales, w_words, w_scales, xo_words, xo_scales, w2_words, w2_scales, sa,
    vs_words, vs_scales, offs, offs2, offs3, offs4, offs5, offs6, out,
):
    nc = tc.nc
    with ExitStack() as ctx:
        lists = ctx.enter_context(tc.tile_pool(name="lists", bufs=1))
        sb = ctx.enter_context(tc.tile_pool(name="sb", bufs=1))
        raw = ctx.enter_context(tc.tile_pool(name="raw", bufs=1))
        mid = ctx.enter_context(tc.tile_pool(name="mid", bufs=1))
        ps = ctx.enter_context(tc.psum_pool(name="ps", bufs=1))

        def load_list(name, src):
            tile = lists.tile(list(src.shape), U16, name=name)
            nc.sync.dma_start(tile[:], src)
            return tile

        def entries(tile, first, last):
            return tile[:, first // LIST_ROWS : last // LIST_ROWS]

        def load_e4m3(name, src, cols, offset, queue):
            tile = raw.tile([P, cols], U32, name=name, offset=offset, align_bytes=64)
            queue.dma_start(tile[:].bitcast(I32), src[0].rearrange("p n t -> p (n t)").bitcast(I32))
            return tile

        def load_e2m1(name, src, cols, offset, queue):
            tile = raw.tile([P, cols], U16, name=name, offset=offset, align_bytes=64)
            queue.dma_start(tile[:].bitcast(I32), src[0].bitcast(I32))
            return tile

        def zeroed_plane(name, cols, offset):
            tile = raw.tile([P, cols], U8, name=name, offset=offset, align_bytes=64)
            nc.vector.memset(tile[:].bitcast(I32), 0)
            return tile

        def load_plane(queue, tile, src):
            rows = src[0].rearrange("(q r) n -> r q n", r=4)
            for r in range(4):
                queue.dma_start(tile[r:P:32, :].bitcast(I32), rows[r].bitcast(I32))

        def bank(b, shape):
            return ps.tile(shape, F32, name=f"bank{b}", tag=f"bank{b}")

        xt_plane = raw.tile([P, T], U8, name="xt_plane", offset=8192, align_bytes=64)
        nc.vector.memset(xt_plane[:, : T // 2].bitcast(I32), 0)
        nc.gpsimd.memset(xt_plane[:, T // 2 :].bitcast(I32), 0)
        w_plane = zeroed_plane("w_plane", R, 10240)
        w_rows = sb.tile([4, 4, R // 4], I32, name="w_rows")
        nc.sync.dma_start(w_rows[:], w_scales[0].rearrange("(q r) n -> r q n", r=4).bitcast(I32))
        w_raw = load_e2m1("w_raw", w_words, R, 10752, nc.scalar)
        xt_raw = load_e4m3("xt_raw", xt_words, T, 0, nc.scalar)
        load_plane(nc.sync, xt_plane, xt_scales)
        idx = load_list("idx", offs)
        idx3 = load_list("idx3", offs3)
        idx4 = load_list("idx4", offs4)
        idx5 = load_list("idx5", offs5)
        idx2 = load_list("idx2", offs2)
        idx6 = load_list("idx6", offs6)

        boards = [sb.tile([P, C], F32, name=f"board{i}") for i in range(2)]
        for board in boards:
            nc.vector.memset(board[:], 0.0)

        for q in range(4):
            nc.vector.tensor_copy(out=w_plane[32 * q : 32 * q + 4, :].bitcast(I32), in_=w_rows[:, q, :])
        w_code = mid.tile([P, PACK, P], U16, name="w_code", offset=2048, align_bytes=64)
        w_scale = mid.tile([P, PACK, P], U8, name="w_scale", offset=3072, align_bytes=64)
        nc.scalar.copy(out=w_code[:], in_=w_raw[:].rearrange("p (m t) -> p t m", t=PACK))
        dealt = w_plane[:].rearrange("p (m t) -> p t m", t=PACK)
        nc.vector.tensor_copy(out=w_scale[:, :2, :], in_=dealt[:, :2, :])

        x_code = mid.tile([P, J], U32, name="x_code", offset=0, align_bytes=64)
        x_scale = mid.tile([P, J], U8, name="x_scale", offset=3584, align_bytes=64)
        nc.vector.tensor_copy(out=x_scale[:, : J // 2], in_=xt_plane[:].indirect(entries(idx, 0, J // 2)))
        nc.vector.tensor_copy(out=x_code[:, :HEAD], in_=xt_raw[:].indirect(entries(idx, 0, HEAD)))
        nc.vector.tensor_copy(out=x_code[:, HEAD : J // 2], in_=xt_raw[:].indirect(entries(idx, HEAD, J // 2)))

        def first_product(dst, t, first, last):
            nc.tensor.matmul_mx(
                dst, lhsT=w_code[:, t, :].bitcast(FP4X4), lhsT_scale=w_scale[:, t, :],
                rhs=x_code[:, first:last].bitcast(FP8X4), rhs_scale=x_scale[:, first:last],
                start=True, stop=True,
            )

        a_head = []
        for t in range(2):
            acc = bank(t, [P, HEAD])
            first_product(acc[:], t, 0, HEAD)
            head = mid.tile([P, HEAD], F32, name=f"a_head{t}", offset=4096 + 512 * t, align_bytes=64)
            nc.scalar.activation(out=head[:], in_=acc[:], func=COPY)
            a_head.append(head)

        acc = bank(2, [P, 2, HEAD])
        for t in range(2):
            first_product(acc[:, t, :], t, HEAD, 2 * HEAD)
        a_next = mid.tile([P, 2, HEAD], F32, name="a_next", offset=5120, align_bytes=64)
        nc.vector.tensor_copy(out=a_next[:], in_=acc[:])
        nc.vector.tensor_copy(out=x_scale[:, J // 2 :], in_=xt_plane[:].indirect(entries(idx, J // 2, J)))
        nc.vector.tensor_copy(out=x_code[:, J // 2 :], in_=xt_raw[:].indirect(entries(idx, J // 2, J)))
        a_rest = []
        for t in range(2):
            acc = bank(3 + t, [P, J // 2])
            first_product(acc[:], t, J // 2, J)
            rest = mid.tile([P, J // 2], F32, name=f"a_rest{t}", offset=6144 + 1024 * t, align_bytes=64)
            nc.vector.tensor_copy(out=rest[:], in_=acc[:])
            a_rest.append(rest)
        nc.vector.tensor_copy(out=w_scale[:, 2:, :], in_=dealt[:, 2:, :])
        for t in range(2, PACK):
            acc = bank(3 + t, [P, J])
            first_product(acc[:], t, 0, J)
            rest = sb.tile([P, J], F32, name=f"a_rest{t}")
            nc.vector.tensor_copy(out=rest[:], in_=acc[:])
            a_rest.append(rest)

        gain = raw.tile([P, PACK], F32, name="gain", offset=10752, align_bytes=64)
        nc.sync.dma_start(gain[:], sa.rearrange("(p t) o -> p (t o)", t=PACK))
        xo_raw = load_e2m1("xo_raw", xo_words, M, 0, nc.sync)
        w2_raw = load_e4m3("w2_raw", w2_words, R, 2048, nc.sync)
        xo_plane = zeroed_plane("xo_plane", M, 8192)
        w2_plane = zeroed_plane("w2_plane", R, 9216)
        vs_plane = zeroed_plane("vs_plane", V, 9728)
        load_plane(nc.sync, xo_plane, xo_scales)
        load_plane(nc.sync, w2_plane, w2_scales)
        load_plane(nc.sync, vs_plane, vs_scales)

        slots = [mid.tile([P, J], F32, name=f"slots{t}", offset=2048 * t, align_bytes=64) for t in range(PACK)]

        o_code = sb.tile([P, J], U16, name="o_code", align_bytes=64)
        o_scale = sb.tile([P, J], U8, name="o_scale", align_bytes=64)
        nc.vector.tensor_copy(out=o_code[:], in_=xo_raw[:].indirect(idx2[:]))
        nc.vector.tensor_copy(out=o_scale[:], in_=xo_plane[:].indirect(idx2[:]))
        w2_code = sb.tile([P, PACK, P], U32, name="w2_code", align_bytes=64)
        w2_scale = sb.tile([P, PACK, P], U8, name="w2_scale", align_bytes=64)
        nc.vector.tensor_copy(out=w2_code[:], in_=w2_raw[:].rearrange("p (m t) -> p t m", t=PACK))
        nc.vector.tensor_copy(out=w2_scale[:], in_=w2_plane[:].rearrange("p (m t) -> p t m", t=PACK))
        vs_raw = load_e4m3("vs_raw", vs_words, V, 4096, nc.sync)
        b_ps = []
        for t in range(PACK):
            acc = bank((7 + t) % 8, [P, J])
            nc.tensor.matmul_mx(
                acc[:], lhsT=w2_code[:, t, :].bitcast(FP8X4), lhsT_scale=w2_scale[:, t, :],
                rhs=o_code[:].bitcast(FP4X4), rhs_scale=o_scale[:], start=True, stop=True,
            )
            b_ps.append(acc)

        v_code = sb.tile([P, N], U32, name="v_code", align_bytes=64)
        v_scale = sb.tile([P, N], U8, name="v_scale", align_bytes=64)
        nc.vector.tensor_copy(out=v_code[:], in_=vs_raw[:].indirect(idx6[:]))
        nc.vector.tensor_copy(out=v_scale[:], in_=vs_plane[:].indirect(idx6[:]))

        fetched = [sb.tile([P, S], F32, name=f"fetched{t}") for t in range(PACK)]
        hid = sb.tile([P, J, PACK], BF16, name="hid", align_bytes=64)

        def put(t, first, last, src):
            nc.scalar.activation(out=boards[t % 2][:].indirect(entries(idx3, first, last)), in_=src, func=COPY)

        def fetch(t):
            nc.scalar.activation(
                out=fetched[t][:], in_=boards[t % 2][:].indirect(idx4[:]), func=COPY, scale=gain[:, t : t + 1]
            )

        def hand_back(t):
            nc.scalar.activation(out=slots[t][:].indirect(idx5[:]), in_=fetched[t][:], func=COPY)

        def larger(t, first, last):
            nc.vector.tensor_tensor(
                out=hid[:, first:last, t], in0=b_ps[t][:, first:last], in1=slots[t][:, first:last], op=MAX
            )

        for t in range(2):
            put(t, 0, HEAD, a_head[t][:])
        for t in range(2):
            put(t, HEAD, 2 * HEAD, a_next[:, t, :])
        for t in range(2):
            put(t, J // 2, J, a_rest[t][:])
        for tile in slots:
            nc.vector.memset(tile[:], 0.0)
        fetch(0)
        fetch(1)
        put(2, 0, J, a_rest[2][:])
        hand_back(0)
        larger(0, 0, J)
        put(3, 0, J, a_rest[3][:])
        hand_back(1)
        larger(1, 0, J)
        fetch(2)
        fetch(3)
        hand_back(2)
        larger(2, 0, J)
        hand_back(3)

        h_code = sb.tile([P, J], U32, name="h_code", align_bytes=64)
        h_scale = sb.tile([P, J], U8, name="h_scale", align_bytes=64)
        blocks = N // P
        chunks = J // TAIL

        def finish(c):
            cols = slice(c * TAIL, (c + 1) * TAIL)
            nc.vector.quantize_mx(
                out=h_code[:, cols].bitcast(FP8X4), scales=h_scale[:, cols],
                in_=hid[:, cols, :].rearrange("p j t -> p (j t)"),
            )

            def product(dst, b):
                rows = slice(b * P, (b + 1) * P)
                nc.tensor.matmul_mx(
                    dst, lhsT=v_code[:, rows].bitcast(FP8X4), lhsT_scale=v_scale[:, rows],
                    rhs=h_code[:, cols].bitcast(FP8X4), rhs_scale=h_scale[:, cols], start=True, stop=True,
                )

            if c < chunks - 1:
                acc = bank(3 + c, [P, blocks, TAIL])
                for b in range(blocks):
                    product(acc[:, b, :], b)
                result = sb.tile([P, blocks, TAIL], F32, name=f"result{c}")
                nc.scalar.activation(out=result[:], in_=acc[:], func=COPY)
                nc.sync.dma_start(out.rearrange("(b p) j -> p b j", p=P)[:, :, cols], result[:])
                return
            for b in range(blocks):
                acc = bank(3 + c + b, [P, TAIL])
                product(acc[:], b)
                result = sb.tile([P, TAIL], F32, name=f"last{b}")
                if b == 0:
                    nc.scalar.activation(out=result[:], in_=acc[:], func=COPY)
                    nc.scalar.dma_start(out[b * P : (b + 1) * P, cols], result[:])
                else:
                    nc.vector.tensor_copy(out=result[:], in_=acc[:])
                    nc.sync.dma_start(out[b * P : (b + 1) * P, cols], result[:])

        half = J // 2
        plain = sb.tile([P, half], BF16, name="plain")
        nc.vector.tensor_tensor(out=plain[:], in0=b_ps[3][:, half:], in1=slots[3][:, half:], op=MAX)
        for c in range(2):
            nc.scalar.copy(out=hid[:, half + c * TAIL : half + (c + 1) * TAIL, 3], in_=plain[:, c * TAIL : (c + 1) * TAIL])
            larger(3, c * TAIL, (c + 1) * TAIL)
        for c in range(chunks):
            finish(c)
